import numpy as np
import ml_dtypes


def mxq(x, axis, fmt="e4m3"):
    dtype, down = {"e4m3": (ml_dtypes.float8_e4m3fn, 7), "e5m2": (ml_dtypes.float8_e5m2, 14)}[fmt]
    v = np.moveaxis(np.asarray(x, np.float32).astype(ml_dtypes.bfloat16).astype(np.float64), axis, -1)
    blocks = v.reshape(v.shape[:-1] + (-1, 32))
    amax = np.abs(blocks).max(-1, keepdims=True)
    byte = np.maximum(np.where(amax > 0, np.frexp(amax)[1] - 1 + 127, 0) - down, 1)
    scale = np.exp2(byte - 127.0)
    codes = (blocks / scale).astype(np.float32).astype(dtype).astype(np.float64)
    return np.moveaxis((codes * scale).reshape(v.shape), -1, axis)


WIDE = False


def mx_kscale(k):
    if not WIDE:
        return np.ones(k)
    levels = np.array([10, -10, 5, -5, 0])
    if k % 512:
        return np.exp2(np.random.permutation(np.resize(levels, k // 32))).repeat(32)
    a = np.empty((k // 512, 16))
    for p in range(k // 512):
        a[p, :8] = np.random.permutation(np.resize(levels, 8))
        for g in range(8):
            far = levels[np.abs(levels - a[p, g]) >= 10]
            a[p, g + 8] = far[np.random.randint(len(far))]
    return np.exp2(a.ravel()).repeat(32)


def f64(x):
    return np.asarray(x).astype(np.float64)


def striped(idx):
    return np.tile(idx.reshape(-1, 16).T, (8, 1)).astype(np.uint16)


def unstriped(offs):
    return offs[:16].T.reshape(-1).astype(np.int64)


E2M1 = np.array([0.0, 0.5, 1.0, 1.5, 2.0, 3.0, 4.0, 6.0, -0.0, -0.5, -1.0, -1.5, -2.0, -3.0, -4.0, -6.0])


def pack_weight(w, fmt):
    k, n = w.shape
    w = f64(np.asarray(w, np.float32).astype(ml_dtypes.bfloat16)).reshape(k // 32, 32, n)
    amax = np.abs(w).max(1)
    if fmt == "e4m3":
        byte = np.frexp(amax)[1] - 1 + 127 - 7
    else:
        mant, ex = np.frexp(amax / 6.0)
        byte = np.where(mant > 0.5, ex, ex - 1) + 127
    byte = np.clip(np.where(amax > 0, byte, 1), 1, 254)
    scaled = (w * np.exp2(127.0 - byte)[:, None, :]).reshape(k, n).astype(np.float32)
    by_word = np.ascontiguousarray(scaled.reshape(k // 512, 128, 4, n).transpose(0, 1, 3, 2))
    if fmt == "e4m3":
        words = by_word.astype(ml_dtypes.float8_e4m3fn).view(np.uint8)
    else:
        c = by_word.astype(ml_dtypes.float4_e2m1fn).view(np.uint8) & 0xF
        words = (c[..., 0::2] | (c[..., 1::2] << 4)).reshape(k // 512, 128, 2 * n)
    return np.ascontiguousarray(words), np.ascontiguousarray(byte.astype(np.uint8).reshape(k // 512, 16, n))


def unpack_weight(words, scales, fmt):
    g, _, n = scales.shape
    words = np.ascontiguousarray(words).reshape(g, 128, n, -1)
    if fmt == "e4m3":
        vals = words.view(ml_dtypes.float8_e4m3fn).astype(np.float64)
    else:
        nib = np.empty((g, 128, n, 4), np.uint8)
        nib[..., 0::2] = words & 0xF
        nib[..., 1::2] = words >> 4
        vals = E2M1[nib]
    vals = vals * np.repeat(np.exp2(scales.astype(np.float64) - 127.0), 8, axis=1)[..., None]
    return vals.transpose(0, 1, 3, 2).reshape(g * 512, n)


def gelu(v):
    return 0.5 * v * (1.0 + np.tanh(np.sqrt(2.0 / np.pi) * (v + 0.044715 * v**3)))


K, K2, T, T3, S, H, T2, P, N = 1024, 512, 2048, 1024, 512, 1024, 2048, 1024, 512


def setup_inputs():
    n = np.random.standard_normal
    s = mx_kscale(K)[:, None]
    s2 = mx_kscale(K2)[:, None]
    u = mx_kscale(H)[:, None]
    perm = np.random.permutation(T2)
    d = {}
    d["tab_words"], d["tab_scales"] = pack_weight(n((K, T)) * s, "e4m3")
    d["tab2_words"], d["tab2_scales"] = pack_weight(n((K2, T3)) * s2, "e4m3")
    d["offs"] = striped(np.random.permutation(T)[:S])
    d["offs2"] = striped(np.random.permutation(T3)[:S])
    d["offs3"] = striped(perm[:S])
    d["offs4"] = striped(perm[S:2 * S])
    d["offs5"] = striped(np.random.permutation(T2)[:P])
    d["w1"] = (2.0 * n((K, H)) / s / K ** 0.5).astype(np.float32)
    d["gain"] = (1.8 * np.exp(0.3 * n(H)) * u[:, 0]).astype(np.float32)
    d["w2_words"], d["w2_scales"] = pack_weight(0.8 * n((K, H)) / s * u.T / K ** 0.5, "e2m1")
    d["w3"] = (1.5 * n((K2, H)) / s2 * u.T / K2 ** 0.5).astype(np.float32)
    d["wg1"] = np.exp(0.3 * n((128, S))).astype(np.float32)
    d["wg2"] = np.exp(0.3 * n((128, S))).astype(np.float32)
    d["page0"] = (n((H, T2)) * u).astype(np.float32)
    d["base"] = (n(H) * u[:, 0]).astype(np.float32)
    d["w4_words"], d["w4_scales"] = pack_weight(n((H, N)) / u / H ** 0.5, "e4m3")
    d["ages"] = np.exp(0.5 * n((N, P))).astype(np.float32)
    return d


def reference(tab_words, tab_scales, tab2_words, tab2_scales, offs, offs2, offs3, offs4, offs5, w1, gain, w2_words, w2_scales, w3, wg1, wg2, page0, base, w4_words, w4_scales, ages):
    v = unpack_weight(tab_words, tab_scales, "e4m3")[:, unstriped(offs)]
    v2 = unpack_weight(tab2_words, tab2_scales, "e4m3")[:, unstriped(offs2)]
    bent = np.tanh(mxq(f64(w1), 0, "e4m3").T @ v)
    h1 = f64(gain)[:, None] * bent + (unpack_weight(w2_words, w2_scales, "e2m1").T @ v)
    h2 = np.abs(mxq(f64(w3), 0, "e4m3").T @ v2)
    page = f64(page0).copy()
    page[:, unstriped(offs3)] = np.tile(f64(wg1), (H // 128, 1)) * h1
    page[:, unstriped(offs4)] = np.tile(f64(wg2), (H // 128, 1)) * h2
    x = mxq(page[:, unstriped(offs5)] - f64(base)[:, None], 0, "e4m3")
    y = unpack_weight(w4_words, w4_scales, "e4m3").T @ x
    return y * f64(ages)

@@ -1,0 +1,305 @@
+from contextlib import ExitStack
+
+import concourse.mybir as mybir
+from concourse.masks import make_identity
+
+K, K2, T, T3, S, H, T2, PICK, N = 1024, 512, 2048, 1024, 512, 1024, 2048, 1024, 512
+FLOPS = 2 * (2 * K * H * S + K2 * H * S + H * N * PICK)
+
+F32 = mybir.dt.float32
+BF16 = mybir.dt.bfloat16
+I32 = mybir.dt.int32
+U32 = mybir.dt.uint32
+U16 = mybir.dt.uint16
+U8 = mybir.dt.uint8
+FP8X4 = mybir.dt.float8_e4m3fn_x4
+FP4X4 = mybir.dt.float4_e2m1fn_x4
+ACT = mybir.ActivationFunctionType
+MULT = mybir.AluOpType.mult
+ADD = mybir.AluOpType.add
+
+P = 128
+PACK = 4
+KP = P * PACK
+CHUNK = 256
+CHUNKS = PICK // CHUNK
+TILES = H // P
+
+
+def tile_list_biofouling_plate_page_kernel(
+    tc, tab_words, tab_scales, tab2_words, tab2_scales, offs, offs2, offs3, offs4, offs5,
+    w1, gain, w2_words, w2_scales, w3, wg1, wg2, page0, base, w4_words, w4_scales, ages, out,
+):
+    nc = tc.nc
+    with ExitStack() as ctx:
+        lists = ctx.enter_context(tc.tile_pool(name="lists", bufs=1))
+        sb = ctx.enter_context(tc.tile_pool(name="sb", bufs=1))
+        psum = ctx.enter_context(tc.psum_pool(name="psum", bufs=2))
+
+        def new_tile(shape, dtype, name, tag=None, bufs=1):
+            return sb.tile(shape, dtype, name=name, tag=tag or name, bufs=bufs, align_bytes=64)
+
+        def load_list(src, name):
+            dst = lists.tile(list(src.shape), U16, name=name)
+            nc.sync.dma_start(dst[:], src)
+            return dst
+
+        def load_words(src, name):
+            dst = new_tile([P, src.shape[1]], U32, name)
+            nc.sync.dma_start(dst[:].bitcast(I32), src.rearrange("p c i -> p (c i)").bitcast(I32))
+            return dst
+
+        def cleared_plane(src, name):
+            dst = new_tile([P, src.shape[0], src.shape[2]], U8, name)
+            nc.vector.memset(dst[:].bitcast(I32), 0)
+            return dst
+
+        def load_scales(dst, src, queue):
+            for q in range(4):
+                queue.dma_start(
+                    dst[32 * q : 32 * q + 4, :, :].bitcast(I32),
+                    src.bitcast(I32)[:, 4 * q : 4 * q + 4, :].rearrange("a r c -> r a c"),
+                )
+
+        def load_weight(w, a, b, slot):
+            raw = new_tile([P, PACK, KP], F32, "raw_w", tag="raw%d" % slot)
+            rows = w[a * KP : (a + 1) * KP, b * KP : (b + 1) * KP]
+            nc.sync.dma_start(raw[:], rows.rearrange("(p j) c -> p j c", j=PACK))
+            return raw
+
+        def load_page(u):
+            b, t = divmod(u, PACK)
+            dst = new_tile([P, T2], F32, "page%d" % u)
+            nc.sync.dma_start(dst[:], page0.rearrange("(b p t) c -> b t p c", p=P, t=PACK)[b, t])
+            return dst
+
+        def load_wg(wg, half, name):
+            dst = new_tile([P, 2, S], F32, name)
+            rows = wg.rearrange("(i t) c -> i t c", t=PACK)[:, 2 * half : 2 * half + 2, :]
+            for q in range(4):
+                nc.sync.dma_start(dst[32 * q : 32 * q + 32, :, :], rows)
+            return dst
+
+        def load_rowvec(v, name):
+            dst = new_tile([P, TILES], F32, name)
+            nc.sync.dma_start(
+                dst[:].rearrange("p (b t) -> p b t", t=PACK), v.rearrange("(b p t) -> p b t", p=P, t=PACK)
+            )
+            return dst
+
+        def gather(window, offsets, dtype, name):
+            dst = new_tile([P, S], dtype, name)
+            nc.vector.tensor_copy(dst[:], window.indirect(offsets[:]))
+            return dst
+
+        def quantize_weight(raw, codes, scales, parts):
+            staged = new_tile([P, PACK * KP], BF16, "staged", tag="stage", bufs=2)
+            src = raw[:].rearrange("p j (m t) -> p m j t", t=PACK)
+            dst = staged[:].rearrange("p (t m j) -> p m j t", t=PACK, j=PACK)
+            for t0, t1 in parts:
+                nc.scalar.copy(dst[:, :, :, t0:t1], src[:, :, :, t0:t1])
+                nc.vector.quantize_mx(
+                    out=codes[:, t0 * P : t1 * P].bitcast(FP8X4),
+                    scales=scales[:, t0 * P : t1 * P],
+                    in_=staged[:, t0 * KP : t1 * KP],
+                )
+
+        def mx(acc, lhs, lhs_s, rhs, rhs_s, start, stop, rhs_dtype=FP8X4):
+            nc.tensor.matmul_mx(
+                out=acc, lhsT=lhs.bitcast(FP8X4), lhsT_scale=lhs_s,
+                rhs=rhs.bitcast(rhs_dtype), rhs_scale=rhs_s, start=start, stop=stop,
+            )
+
+        whole = [(0, PACK)]
+        pages = {}
+
+        o2 = load_list(offs2, "o2")
+        t2s = cleared_plane(tab2_scales, "t2s")
+        t1s = cleared_plane(tab_scales, "t1s")
+        w2s = cleared_plane(w2_scales, "w2s")
+        w4s = cleared_plane(w4_scales, "w4s")
+        load_scales(t2s, tab2_scales, nc.scalar)
+        load_scales(t1s, tab_scales, nc.gpsimd)
+        load_scales(w2s, w2_scales, nc.gpsimd)
+        t2w = load_words(tab2_words[0], "t2w")
+        raw3 = [load_weight(w3, 0, 0, 0)]
+        wg2_sb = [load_wg(wg2, 0, "wg2lo")]
+        o4 = load_list(offs4, "o4")
+        pages[0] = load_page(0)
+        o1 = load_list(offs, "o1")
+        ident = new_tile([P, P], F32, "ident")
+        make_identity(nc, ident[:])
+
+        v2s = gather(t2s[:, 0, :], o2, U8, "v2s")
+        v2w = gather(t2w[:], o2, U32, "v2w")
+        v1s = [gather(t1s[:, a, :], o1, U8, "v1s%d" % a) for a in range(2)]
+
+        w3c = [new_tile([P, KP], U32, "w3c%d" % b) for b in range(2)]
+        w3s = [new_tile([P, KP], U8, "w3s%d" % b) for b in range(2)]
+        w1c = [[new_tile([P, KP], U32, "w1c%d%d" % (b, a)) for a in range(2)] for b in range(2)]
+        w1s = [[new_tile([P, KP], U8, "w1s%d%d" % (b, a)) for a in range(2)] for b in range(2)]
+        quantize_weight(raw3[0], w3c[0], w3s[0], [(0, 1), (1, PACK)])
+
+        def put_h2(u):
+            b, t = divmod(u, PACK)
+            cols = slice(t * P, (t + 1) * P)
+            acc = psum.tile([P, S], F32, name="acc_h2", tag="pc")
+            mx(acc[:], w3c[b][:, cols], w3s[b][:, cols], v2w[:], v2s[:], True, True)
+            h2 = new_tile([P, S], F32, "h2", bufs=3)
+            nc.scalar.activation(h2[:], acc[:], ACT.Abs)
+            nc.vector.tensor_tensor(pages[u][:].indirect(o4[:]), h2[:], wg2_sb[t // 2][:, t % 2, :], MULT)
+
+        put_h2(0)
+        pages[1] = load_page(1)
+        put_h2(1)
+        wg2_sb.append(load_wg(wg2, 1, "wg2hi"))
+        pages[2] = load_page(2)
+        put_h2(2)
+        raw3.append(load_weight(w3, 0, 1, 1))
+        t1w = [load_words(tab_words[0], "t1w0")]
+        v1w = [gather(t1w[0][:], o1, U32, "v1w0")]
+        quantize_weight(raw3[1], w3c[1], w3s[1], whole)
+        pages[3] = load_page(3)
+        put_h2(3)
+        t1w.append(load_words(tab_words[1], "t1w1"))
+        v1w.append(gather(t1w[1][:], o1, U32, "v1w1"))
+        pages[4] = load_page(4)
+        put_h2(4)
+
+        w2w = new_tile([P, 2, 2 * H], U8, "w2w")
+        nc.sync.dma_start(w2w[:].bitcast(I32), w2_words.bitcast(I32).rearrange("a p c -> p a c"))
+        gain_sb = load_rowvec(gain, "gain_sb")
+        base_sb = load_rowvec(base, "base_sb")
+        neg_base = new_tile([P, TILES], F32, "neg_base")
+        nc.scalar.mul(neg_base[:], base_sb[:], -1.0)
+        lin_t = []
+        for b in range(2):
+            row = []
+            for jb in range(S // P):
+                acc = psum.tile([P, KP], F32, name="acc_lin_t", tag="pt")
+                picks = slice(jb * P, (jb + 1) * P)
+                for a in range(2):
+                    mx(acc[:], v1w[a][:, picks], v1s[a][:, picks],
+                       w2w[:, a, 2 * b * KP : 2 * (b + 1) * KP], w2s[:, a, b * KP : (b + 1) * KP],
+                       a == 0, a == 1, FP4X4)
+                dst = new_tile([P, PACK, P], F32, "lin_t%d%d" % (b, jb))
+                nc.scalar.copy(dst[:], acc[:].rearrange("p (m t) -> p t m", t=PACK))
+                row.append(dst)
+            lin_t.append(row)
+
+        pages[5] = load_page(5)
+        put_h2(5)
+        quantize_weight(load_weight(w1, 0, 0, 2), w1c[0][0], w1s[0][0], whole)
+        pages[6] = load_page(6)
+        put_h2(6)
+        quantize_weight(load_weight(w1, 1, 0, 3), w1c[0][1], w1s[0][1], whole)
+        pages[7] = load_page(7)
+        put_h2(7)
+        o3 = load_list(offs3, "o3")
+        wg1_sb = [load_wg(wg1, 0, "wg1lo")]
+        raw1 = [load_weight(w1, a, 1, a) for a in range(2)]
+        o5 = load_list(offs5, "o5")
+        wg1_sb.append(load_wg(wg1, 1, "wg1hi"))
+        w4w = new_tile([P, 2, N], U32, "w4w")
+        nc.sync.dma_start(w4w[:].bitcast(I32), w4_words.rearrange("a p c i -> p a (c i)").bitcast(I32))
+        load_scales(w4s, w4_scales, nc.sync)
+
+        def make_h1(u):
+            b, t = divmod(u, PACK)
+            cols = slice(t * P, (t + 1) * P)
+            acc = psum.tile([P, S], F32, name="acc_h1", tag="pa")
+            for a in range(2):
+                mx(acc[:], w1c[b][a][:, cols], w1s[b][a][:, cols], v1w[a][:], v1s[a][:], a == 0, a == 1)
+            bent = new_tile([P, S], F32, "bent", bufs=2)
+            nc.scalar.activation(bent[:], acc[:], ACT.Tanh)
+            lin = psum.tile([P, S], F32, name="lin", tag="pb")
+            for jb in range(S // P):
+                nc.tensor.transpose(lin[:, jb * P : (jb + 1) * P], lin_t[b][jb][:, t, :], ident[:])
+            h1 = new_tile([P, S], F32, "h1", bufs=2)
+            nc.vector.scalar_tensor_tensor(h1[:], bent[:], gain_sb[:, u : u + 1], lin[:], MULT, ADD)
+            return h1
+
+        xb0 = new_tile([P, PICK, PACK], BF16, "xb0")
+        xb1 = [new_tile([P, CHUNK, PACK], BF16, "xb1_%d" % c) for c in range(CHUNKS)]
+
+        def round_x(dst, src, u):
+            nc.scalar.activation(dst, src, ACT.Identity, bias=neg_base[:, u : u + 1])
+
+        h1_next = make_h1(0)
+        for u in range(TILES):
+            b, t = divmod(u, PACK)
+            h1 = h1_next
+            if u == PACK - 1:
+                for a in range(2):
+                    quantize_weight(raw1[a], w1c[1][a], w1s[1][a], whole)
+            if u + 1 < TILES:
+                h1_next = make_h1(u + 1)
+            nc.vector.tensor_tensor(pages[u][:].indirect(o3[:]), h1[:], wg1_sb[t // 2][:, t % 2, :], MULT)
+            if u == 0:
+                continue
+            if u == PACK - 1:
+                todo = range(PACK)
+            elif u < PACK - 1 or u == TILES - 1:
+                todo = []
+            else:
+                todo = [u]
+            for g in todo:
+                picked = new_tile([P, PICK], F32, "picked", tag="raw%d" % ((1, 0, 2, 3)[g % 4]))
+                nc.vector.tensor_copy(picked[:], pages[g][:].indirect(o5[:]))
+                if g < PACK:
+                    round_x(xb0[:, :, g], picked[:], g)
+                else:
+                    for c in range(CHUNKS):
+                        round_x(xb1[c][:, :, g - PACK], picked[:, c * CHUNK : (c + 1) * CHUNK], g)
+            if u == PACK + 1:
+                x0c = new_tile([P, PICK], U32, "x0c", tag="wg1lo")
+                x0s = new_tile([P, PICK], U8, "x0s")
+                nc.vector.quantize_mx(
+                    out=x0c[:].bitcast(FP8X4), scales=x0s[:], in_=xb0[:].rearrange("p c t -> p (c t)")
+                )
+
+        ages_sb = []
+        for c, (tag, bufs) in enumerate((("wg2lo", 1), ("wg2hi", 1), ("stage", 2), ("stage", 2))):
+            dst = new_tile([P, N // P, CHUNK], F32, "ages_sb", tag=tag, bufs=bufs)
+            nc.sync.dma_start(dst[:], ages[:, c * CHUNK : (c + 1) * CHUNK].rearrange("(n p) j -> p n j", p=P))
+            ages_sb.append(dst)
+
+        y = []
+        for c, tag in enumerate(("pc", "pt", "pa", "pb")):
+            cols = slice(c * CHUNK, (c + 1) * CHUNK)
+            pair = []
+            for h in range(2):
+                acc = psum.tile([P, 2, CHUNK], F32, name="acc_y", tag=tag)
+                for i in range(2):
+                    chans = slice((2 * h + i) * P, (2 * h + i + 1) * P)
+                    mx(acc[:, i, :], w4w[:, 0, chans], w4s[:, 0, chans], x0c[:, cols], x0s[:, cols], i == 0, False)
+                pair.append(acc)
+            y.append(pair)
+
+        last = TILES - 1
+        picked = new_tile([P, PICK], F32, "picked", tag="raw3")
+        per_chunk = CHUNK // 16
+        for c in range(CHUNKS):
+            cols = slice(c * CHUNK, (c + 1) * CHUNK)
+            nc.vector.tensor_copy(
+                picked[:, cols], pages[last][:].indirect(o5[:, c * per_chunk : (c + 1) * per_chunk])
+            )
+            round_x(xb1[c][:, :, PACK - 1], picked[:, cols], last)
+        for c in range(CHUNKS):
+            x1c = new_tile([P, CHUNK], U32, "x1c%d" % c)
+            x1s = new_tile([P, CHUNK], U8, "x1s%d" % c)
+            nc.vector.quantize_mx(
+                out=x1c[:].bitcast(FP8X4), scales=x1s[:], in_=xb1[c][:].rearrange("p c t -> p (c t)")
+            )
+            for h in range(2):
+                for i in range(2):
+                    chans = slice((2 * h + i) * P, (2 * h + i + 1) * P)
+                    mx(y[c][h][:, i, :], w4w[:, 1, chans], w4s[:, 1, chans], x1c[:], x1s[:], False, i == 1)
+        for c in range(CHUNKS):
+            cols = slice(c * CHUNK, (c + 1) * CHUNK)
+            for h in range(2):
+                scored = ages_sb[c][:, 2 * h : 2 * h + 2, :]
+                nc.vector.tensor_tensor(scored, y[c][h][:], scored, MULT)
+                nc.sync.dma_start(
+                    out[2 * h * P : (2 * h + 2) * P, cols].rearrange("(n p) j -> p n j", p=P), scored
+                )

@@ -73,11 +73,14 @@ def tile_list_biofouling_plate_page_kernel(
             nc.sync.dma_start(dst[:], page0.rearrange("(b p t) c -> b t p c", p=P, t=PACK)[b, t])
             return dst
 
-        def load_wg(wg, half, name):
-            dst = new_tile([P, 2, S], F32, name)
-            rows = wg.rearrange("(i t) c -> i t c", t=PACK)[:, 2 * half : 2 * half + 2, :]
+        def load_wg_rows(dst, wg, t0):
+            rows = wg.rearrange("(i t) c -> i t c", t=PACK)[:, t0 : t0 + dst.shape[1], :]
             for q in range(4):
                 nc.sync.dma_start(dst[32 * q : 32 * q + 32, :, :], rows)
+
+        def load_wg(wg, half, name):
+            dst = new_tile([P, 2, S], F32, name)
+            load_wg_rows(dst[:], wg, 2 * half)
             return dst
 
         def load_rowvec(v, name):
@@ -114,19 +117,20 @@ def tile_list_biofouling_plate_page_kernel(
         pages = {}
 
         o2 = load_list(offs2, "o2")
+        o1 = load_list(offs, "o1")
+        o4 = load_list(offs4, "o4")
         t2s = cleared_plane(tab2_scales, "t2s")
         t1s = cleared_plane(tab_scales, "t1s")
         w2s = cleared_plane(w2_scales, "w2s")
         w4s = cleared_plane(w4_scales, "w4s")
         load_scales(t2s, tab2_scales, nc.scalar)
         load_scales(t1s, tab_scales, nc.gpsimd)
-        load_scales(w2s, w2_scales, nc.gpsimd)
-        t2w = load_words(tab2_words[0], "t2w")
         raw3 = [load_weight(w3, 0, 0, 0)]
-        wg2_sb = [load_wg(wg2, 0, "wg2lo")]
-        o4 = load_list(offs4, "o4")
+        t2w = load_words(tab2_words[0], "t2w")
+        wg2_sb = [new_tile([P, 2, S], F32, "wg2lo")]
+        load_wg_rows(wg2_sb[0][:, 0:1, :], wg2, 0)
         pages[0] = load_page(0)
-        o1 = load_list(offs, "o1")
+        load_wg_rows(wg2_sb[0][:, 1:2, :], wg2, 1)
         ident = new_tile([P, P], F32, "ident")
         make_identity(nc, ident[:])
 
@@ -140,40 +144,37 @@ def tile_list_biofouling_plate_page_kernel(
         w1s = [[new_tile([P, KP], U8, "w1s%d%d" % (b, a)) for a in range(2)] for b in range(2)]
         quantize_weight(raw3[0], w3c[0], w3s[0], [(0, 1), (1, PACK)])
 
+        h2_first = new_tile([P, PACK, S], F32, "h2_first", tag="xb0")
+        h2 = [h2_first[:, t, :] for t in range(PACK)]
+        h2.extend(new_tile([P, S], F32, "h2_second", tag="xb1_%d" % t)[:] for t in range(PACK))
+
         def put_h2(u):
             b, t = divmod(u, PACK)
             cols = slice(t * P, (t + 1) * P)
             acc = psum.tile([P, S], F32, name="acc_h2", tag="pc")
             mx(acc[:], w3c[b][:, cols], w3s[b][:, cols], v2w[:], v2s[:], True, True)
-            h2 = new_tile([P, S], F32, "h2", bufs=3)
-            nc.scalar.activation(h2[:], acc[:], ACT.Abs)
-            nc.vector.tensor_tensor(pages[u][:].indirect(o4[:]), h2[:], wg2_sb[t // 2][:, t % 2, :], MULT)
+            nc.scalar.activation(h2[u], acc[:], ACT.Abs)
+            nc.vector.tensor_tensor(pages[u][:].indirect(o4[:]), h2[u], wg2_sb[t // 2][:, t % 2, :], MULT)
 
         put_h2(0)
         pages[1] = load_page(1)
         put_h2(1)
         wg2_sb.append(load_wg(wg2, 1, "wg2hi"))
-        pages[2] = load_page(2)
-        put_h2(2)
-        raw3.append(load_weight(w3, 0, 1, 1))
         t1w = [load_words(tab_words[0], "t1w0")]
         v1w = [gather(t1w[0][:], o1, U32, "v1w0")]
-        quantize_weight(raw3[1], w3c[1], w3s[1], whole)
-        pages[3] = load_page(3)
-        put_h2(3)
+        pages[2] = load_page(2)
+        put_h2(2)
+        quantize_weight(load_weight(w3, 0, 1, 1), w3c[1], w3s[1], whole)
         t1w.append(load_words(tab_words[1], "t1w1"))
         v1w.append(gather(t1w[1][:], o1, U32, "v1w1"))
-        pages[4] = load_page(4)
-        put_h2(4)
+        pages[3] = load_page(3)
+        put_h2(3)
 
         w2w = new_tile([P, 2, 2 * H], U8, "w2w")
         nc.sync.dma_start(w2w[:].bitcast(I32), w2_words.bitcast(I32).rearrange("a p c -> p a c"))
-        gain_sb = load_rowvec(gain, "gain_sb")
-        base_sb = load_rowvec(base, "base_sb")
-        neg_base = new_tile([P, TILES], F32, "neg_base")
-        nc.scalar.mul(neg_base[:], base_sb[:], -1.0)
-        lin_t = []
-        for b in range(2):
+        load_scales(w2s, w2_scales, nc.sync)
+
+        def make_lin_t(b):
             row = []
             for jb in range(S // P):
                 acc = psum.tile([P, KP], F32, name="acc_lin_t", tag="pt")
@@ -182,17 +183,25 @@ def tile_list_biofouling_plate_page_kernel(
                     mx(acc[:], v1w[a][:, picks], v1s[a][:, picks],
                        w2w[:, a, 2 * b * KP : 2 * (b + 1) * KP], w2s[:, a, b * KP : (b + 1) * KP],
                        a == 0, a == 1, FP4X4)
-                dst = new_tile([P, PACK, P], F32, "lin_t%d%d" % (b, jb))
+                dst = new_tile([P, PACK, P], F32, "lin_t%d" % jb)
                 nc.scalar.copy(dst[:], acc[:].rearrange("p (m t) -> p t m", t=PACK))
                 row.append(dst)
-            lin_t.append(row)
+            return row
 
+        lin_t = [make_lin_t(0)]
+        pages[4] = load_page(4)
+        put_h2(4)
+        raw = load_weight(w1, 0, 0, 2)
         pages[5] = load_page(5)
         put_h2(5)
-        quantize_weight(load_weight(w1, 0, 0, 2), w1c[0][0], w1s[0][0], whole)
+        quantize_weight(raw, w1c[0][0], w1s[0][0], whole)
+        quantize_weight(load_weight(w1, 1, 0, 3), w1c[0][1], w1s[0][1], whole)
+        gain_sb = load_rowvec(gain, "gain_sb")
+        base_sb = load_rowvec(base, "base_sb")
+        neg_base = new_tile([P, TILES], F32, "neg_base")
+        nc.scalar.mul(neg_base[:], base_sb[:], -1.0)
         pages[6] = load_page(6)
         put_h2(6)
-        quantize_weight(load_weight(w1, 1, 0, 3), w1c[0][1], w1s[0][1], whole)
         pages[7] = load_page(7)
         put_h2(7)
         o3 = load_list(offs3, "o3")
@@ -230,6 +239,7 @@ def tile_list_biofouling_plate_page_kernel(
             b, t = divmod(u, PACK)
             h1 = h1_next
             if u == PACK - 1:
+                lin_t.append(make_lin_t(1))
                 for a in range(2):
                     quantize_weight(raw1[a], w1c[1][a], w1s[1][a], whole)
             if u + 1 < TILES:

@@ -75,7 +75,7 @@ def tile_list_biofouling_plate_page_kernel(
 
         def load_wg_rows(dst, wg, t0):
             rows = wg.rearrange("(i t) c -> i t c", t=PACK)[:, t0 : t0 + dst.shape[1], :]
-            for q in range(4):
+            for q in (0, 2, 1, 3):
                 nc.sync.dma_start(dst[32 * q : 32 * q + 32, :, :], rows)
 
         def load_wg(wg, half, name):
@@ -144,7 +144,7 @@ def tile_list_biofouling_plate_page_kernel(
         w1s = [[new_tile([P, KP], U8, "w1s%d%d" % (b, a)) for a in range(2)] for b in range(2)]
         quantize_weight(raw3[0], w3c[0], w3s[0], [(0, 1), (1, PACK)])
 
-        h2_first = new_tile([P, PACK, S], F32, "h2_first", tag="xb0")
+        h2_first = new_tile([P, PACK, S], F32, "h2_first")
         h2 = [h2_first[:, t, :] for t in range(PACK)]
         h2.extend(new_tile([P, S], F32, "h2_second", tag="xb1_%d" % t)[:] for t in range(PACK))
 
@@ -213,54 +213,60 @@ def tile_list_biofouling_plate_page_kernel(
         nc.sync.dma_start(w4w[:].bitcast(I32), w4_words.rearrange("a p c i -> p a (c i)").bitcast(I32))
         load_scales(w4s, w4_scales, nc.sync)
 
+        pick_slots = ("raw2", "raw3", "raw0")
+
         def make_h1(u):
             b, t = divmod(u, PACK)
             cols = slice(t * P, (t + 1) * P)
             acc = psum.tile([P, S], F32, name="acc_h1", tag="pa")
             for a in range(2):
                 mx(acc[:], w1c[b][a][:, cols], w1s[b][a][:, cols], v1w[a][:], v1s[a][:], a == 0, a == 1)
-            bent = new_tile([P, S], F32, "bent", bufs=2)
+            if u == 2:
+                bent = new_tile([P, S], F32, "bent", tag="raw1")
+            elif u < PACK:
+                bent = new_tile([P, S], F32, "bent", bufs=2)
+            else:
+                bent = new_tile([P, S], F32, "bent", tag=pick_slots[(u - PACK) % 3])
             nc.scalar.activation(bent[:], acc[:], ACT.Tanh)
             lin = psum.tile([P, S], F32, name="lin", tag="pb")
             for jb in range(S // P):
                 nc.tensor.transpose(lin[:, jb * P : (jb + 1) * P], lin_t[b][jb][:, t, :], ident[:])
             h1 = new_tile([P, S], F32, "h1", bufs=2)
-            nc.vector.scalar_tensor_tensor(h1[:], bent[:], gain_sb[:, u : u + 1], lin[:], MULT, ADD)
+            if u < 3:
+                nc.vector.scalar_tensor_tensor(h1[:], bent[:], gain_sb[:, u : u + 1], lin[:], MULT, ADD)
+            else:
+                lin_sb = new_tile([P, S], F32, "lin_sb", bufs=2)
+                nc.scalar.copy(lin_sb[:], lin[:])
+                nc.gpsimd.tensor_scalar(h1[:], bent[:], gain_sb[:, u : u + 1], 0.0, MULT, ADD)
+                nc.gpsimd.tensor_tensor(h1[:], h1[:], lin_sb[:], ADD)
             return h1
 
-        xb0 = new_tile([P, PICK, PACK], BF16, "xb0")
         xb1 = [new_tile([P, CHUNK, PACK], BF16, "xb1_%d" % c) for c in range(CHUNKS)]
 
         def round_x(dst, src, u):
             nc.scalar.activation(dst, src, ACT.Identity, bias=neg_base[:, u : u + 1])
 
-        h1_next = make_h1(0)
+        h1 = [make_h1(0), make_h1(1)]
         for u in range(TILES):
-            b, t = divmod(u, PACK)
-            h1 = h1_next
-            if u == PACK - 1:
-                lin_t.append(make_lin_t(1))
+            t = u % PACK
+            nc.vector.tensor_tensor(pages[u][:].indirect(o3[:]), h1[u][:], wg1_sb[t // 2][:, t % 2, :], MULT)
+            if u == 0:
                 for a in range(2):
                     quantize_weight(raw1[a], w1c[1][a], w1s[1][a], whole)
-            if u + 1 < TILES:
-                h1_next = make_h1(u + 1)
-            nc.vector.tensor_tensor(pages[u][:].indirect(o3[:]), h1[:], wg1_sb[t // 2][:, t % 2, :], MULT)
+            if u == 2:
+                lin_t.append(make_lin_t(1))
+            if u + 2 < TILES:
+                h1.append(make_h1(u + 2))
             if u == 0:
-                continue
-            if u == PACK - 1:
-                todo = range(PACK)
-            elif u < PACK - 1 or u == TILES - 1:
-                todo = []
-            else:
-                todo = [u]
-            for g in todo:
-                picked = new_tile([P, PICK], F32, "picked", tag="raw%d" % ((1, 0, 2, 3)[g % 4]))
-                nc.vector.tensor_copy(picked[:], pages[g][:].indirect(o5[:]))
-                if g < PACK:
-                    round_x(xb0[:, :, g], picked[:], g)
+                xb0 = new_tile([P, PICK, PACK], BF16, "xb0", tag="raw1")
+            if u < TILES - 1:
+                picked = new_tile([P, PICK], F32, "picked", tag=pick_slots[u % 3])
+                nc.vector.tensor_copy(picked[:], pages[u][:].indirect(o5[:]))
+                if u < PACK:
+                    round_x(xb0[:, :, u], picked[:], u)
                 else:
                     for c in range(CHUNKS):
-                        round_x(xb1[c][:, :, g - PACK], picked[:, c * CHUNK : (c + 1) * CHUNK], g)
+                        round_x(xb1[c][:, :, t], picked[:, c * CHUNK : (c + 1) * CHUNK], u)
             if u == PACK + 1:
                 x0c = new_tile([P, PICK], U32, "x0c", tag="wg1lo")
                 x0s = new_tile([P, PICK], U8, "x0s")
@@ -287,7 +293,7 @@ def tile_list_biofouling_plate_page_kernel(
             y.append(pair)
 
         last = TILES - 1
-        picked = new_tile([P, PICK], F32, "picked", tag="raw3")
+        picked = new_tile([P, PICK], F32, "picked", tag=pick_slots[last % 3])
         per_chunk = CHUNK // 16
         for c in range(CHUNKS):
             cols = slice(c * CHUNK, (c + 1) * CHUNK)

from contextlib import ExitStack

import concourse.mybir as mybir
from concourse.masks import make_identity

K, K2, T, T3, S, H, T2, PICK, N = 1024, 512, 2048, 1024, 512, 1024, 2048, 1024, 512
FLOPS = 2 * (2 * K * H * S + K2 * H * S + H * N * PICK)

F32 = mybir.dt.float32
BF16 = mybir.dt.bfloat16
I32 = mybir.dt.int32
U32 = mybir.dt.uint32
U16 = mybir.dt.uint16
U8 = mybir.dt.uint8
FP8X4 = mybir.dt.float8_e4m3fn_x4
FP4X4 = mybir.dt.float4_e2m1fn_x4
ACT = mybir.ActivationFunctionType
MULT = mybir.AluOpType.mult
ADD = mybir.AluOpType.add

P = 128
PACK = 4
KP = P * PACK
CHUNK = 256
CHUNKS = PICK // CHUNK
TILES = H // P


def tile_list_biofouling_plate_page_kernel(
    tc, tab_words, tab_scales, tab2_words, tab2_scales, offs, offs2, offs3, offs4, offs5,
    w1, gain, w2_words, w2_scales, w3, wg1, wg2, page0, base, w4_words, w4_scales, ages, out,
):
    nc = tc.nc
    with ExitStack() as ctx:
        lists = ctx.enter_context(tc.tile_pool(name="lists", bufs=1))
        sb = ctx.enter_context(tc.tile_pool(name="sb", bufs=1))
        psum = ctx.enter_context(tc.psum_pool(name="psum", bufs=2))

        def new_tile(shape, dtype, name, tag=None, bufs=1):
            return sb.tile(shape, dtype, name=name, tag=tag or name, bufs=bufs, align_bytes=64)

        def load_list(src, name):
            dst = lists.tile(list(src.shape), U16, name=name)
            nc.sync.dma_start(dst[:], src)
            return dst

        def load_words(src, name):
            dst = new_tile([P, src.shape[1]], U32, name)
            nc.sync.dma_start(dst[:].bitcast(I32), src.rearrange("p c i -> p (c i)").bitcast(I32))
            return dst

        def cleared_plane(src, name):
            dst = new_tile([P, src.shape[0], src.shape[2]], U8, name)
            nc.vector.memset(dst[:].bitcast(I32), 0)
            return dst

        def load_scales(dst, src, queue):
            for q in range(4):
                queue.dma_start(
                    dst[32 * q : 32 * q + 4, :, :].bitcast(I32),
                    src.bitcast(I32)[:, 4 * q : 4 * q + 4, :].rearrange("a r c -> r a c"),
                )

        def load_weight(w, a, b, slot):
            raw = new_tile([P, PACK, KP], F32, "raw_w", tag="raw%d" % slot)
            rows = w[a * KP : (a + 1) * KP, b * KP : (b + 1) * KP]
            nc.sync.dma_start(raw[:], rows.rearrange("(p j) c -> p j c", j=PACK))
            return raw

        def load_page(u):
            b, t = divmod(u, PACK)
            dst = new_tile([P, T2], F32, "page%d" % u)
            nc.sync.dma_start(dst[:], page0.rearrange("(b p t) c -> b t p c", p=P, t=PACK)[b, t])
            return dst

        def load_wg_rows(dst, wg, t0):
            rows = wg.rearrange("(i t) c -> i t c", t=PACK)[:, t0 : t0 + dst.shape[1], :]
            for q in (0, 2, 1, 3):
                nc.sync.dma_start(dst[32 * q : 32 * q + 32, :, :], rows)

        def load_wg(wg, half, name):
            dst = new_tile([P, 2, S], F32, name)
            load_wg_rows(dst[:], wg, 2 * half)
            return dst

        def load_rowvec(v, name):
            dst = new_tile([P, TILES], F32, name)
            nc.sync.dma_start(
                dst[:].rearrange("p (b t) -> p b t", t=PACK), v.rearrange("(b p t) -> p b t", p=P, t=PACK)
            )
            return dst

        def gather(window, offsets, dtype, name):
            dst = new_tile([P, S], dtype, name)
            nc.vector.tensor_copy(dst[:], window.indirect(offsets[:]))
            return dst

        def quantize_weight(raw, codes, scales, parts):
            staged = new_tile([P, PACK * KP], BF16, "staged", tag="stage", bufs=2)
            src = raw[:].rearrange("p j (m t) -> p m j t", t=PACK)
            dst = staged[:].rearrange("p (t m j) -> p m j t", t=PACK, j=PACK)
            for t0, t1 in parts:
                nc.scalar.copy(dst[:, :, :, t0:t1], src[:, :, :, t0:t1])
                nc.vector.quantize_mx(
                    out=codes[:, t0 * P : t1 * P].bitcast(FP8X4),
                    scales=scales[:, t0 * P : t1 * P],
                    in_=staged[:, t0 * KP : t1 * KP],
                )

        def mx(acc, lhs, lhs_s, rhs, rhs_s, start, stop, rhs_dtype=FP8X4):
            nc.tensor.matmul_mx(
                out=acc, lhsT=lhs.bitcast(FP8X4), lhsT_scale=lhs_s,
                rhs=rhs.bitcast(rhs_dtype), rhs_scale=rhs_s, start=start, stop=stop,
            )

        whole = [(0, PACK)]
        pages = {}

        o2 = load_list(offs2, "o2")
        o1 = load_list(offs, "o1")
        o4 = load_list(offs4, "o4")
        t2s = cleared_plane(tab2_scales, "t2s")
        t1s = cleared_plane(tab_scales, "t1s")
        w2s = cleared_plane(w2_scales, "w2s")
        w4s = cleared_plane(w4_scales, "w4s")
        load_scales(t2s, tab2_scales, nc.scalar)
        load_scales(t1s, tab_scales, nc.gpsimd)
        raw3 = [load_weight(w3, 0, 0, 0)]
        t2w = load_words(tab2_words[0], "t2w")
        wg2_sb = [new_tile([P, 2, S], F32, "wg2lo")]
        load_wg_rows(wg2_sb[0][:, 0:1, :], wg2, 0)
        pages[0] = load_page(0)
        load_wg_rows(wg2_sb[0][:, 1:2, :], wg2, 1)
        ident = new_tile([P, P], F32, "ident")
        make_identity(nc, ident[:])

        v2s = gather(t2s[:, 0, :], o2, U8, "v2s")
        v2w = gather(t2w[:], o2, U32, "v2w")
        v1s = [gather(t1s[:, a, :], o1, U8, "v1s%d" % a) for a in range(2)]

        w3c = [new_tile([P, KP], U32, "w3c%d" % b) for b in range(2)]
        w3s = [new_tile([P, KP], U8, "w3s%d" % b) for b in range(2)]
        w1c = [[new_tile([P, KP], U32, "w1c%d%d" % (b, a)) for a in range(2)] for b in range(2)]
        w1s = [[new_tile([P, KP], U8, "w1s%d%d" % (b, a)) for a in range(2)] for b in range(2)]
        quantize_weight(raw3[0], w3c[0], w3s[0], [(0, 1), (1, PACK)])

        h2_first = new_tile([P, PACK, S], F32, "h2_first")
        h2 = [h2_first[:, t, :] for t in range(PACK)]
        h2.extend(new_tile([P, S], F32, "h2_second", tag="xb1_%d" % t)[:] for t in range(PACK))

        def put_h2(u):
            b, t = divmod(u, PACK)
            cols = slice(t * P, (t + 1) * P)
            acc = psum.tile([P, S], F32, name="acc_h2", tag="pc")
            mx(acc[:], w3c[b][:, cols], w3s[b][:, cols], v2w[:], v2s[:], True, True)
            nc.scalar.activation(h2[u], acc[:], ACT.Abs)
            nc.vector.tensor_tensor(pages[u][:].indirect(o4[:]), h2[u], wg2_sb[t // 2][:, t % 2, :], MULT)

        put_h2(0)
        pages[1] = load_page(1)
        put_h2(1)
        wg2_sb.append(load_wg(wg2, 1, "wg2hi"))
        t1w = [load_words(tab_words[0], "t1w0")]
        v1w = [gather(t1w[0][:], o1, U32, "v1w0")]
        pages[2] = load_page(2)
        put_h2(2)
        quantize_weight(load_weight(w3, 0, 1, 1), w3c[1], w3s[1], whole)
        t1w.append(load_words(tab_words[1], "t1w1"))
        v1w.append(gather(t1w[1][:], o1, U32, "v1w1"))
        pages[3] = load_page(3)
        put_h2(3)

        w2w = new_tile([P, 2, 2 * H], U8, "w2w")
        nc.sync.dma_start(w2w[:].bitcast(I32), w2_words.bitcast(I32).rearrange("a p c -> p a c"))
        load_scales(w2s, w2_scales, nc.sync)

        def make_lin_t(b):
            row = []
            for jb in range(S // P):
                acc = psum.tile([P, KP], F32, name="acc_lin_t", tag="pt")
                picks = slice(jb * P, (jb + 1) * P)
                for a in range(2):
                    mx(acc[:], v1w[a][:, picks], v1s[a][:, picks],
                       w2w[:, a, 2 * b * KP : 2 * (b + 1) * KP], w2s[:, a, b * KP : (b + 1) * KP],
                       a == 0, a == 1, FP4X4)
                dst = new_tile([P, PACK, P], F32, "lin_t%d" % jb)
                nc.scalar.copy(dst[:], acc[:].rearrange("p (m t) -> p t m", t=PACK))
                row.append(dst)
            return row

        lin_t = [make_lin_t(0)]
        pages[4] = load_page(4)
        put_h2(4)
        raw = load_weight(w1, 0, 0, 2)
        pages[5] = load_page(5)
        put_h2(5)
        quantize_weight(raw, w1c[0][0], w1s[0][0], whole)
        quantize_weight(load_weight(w1, 1, 0, 3), w1c[0][1], w1s[0][1], whole)
        gain_sb = load_rowvec(gain, "gain_sb")
        base_sb = load_rowvec(base, "base_sb")
        neg_base = new_tile([P, TILES], F32, "neg_base")
        nc.scalar.mul(neg_base[:], base_sb[:], -1.0)
        pages[6] = load_page(6)
        put_h2(6)
        pages[7] = load_page(7)
        put_h2(7)
        o3 = load_list(offs3, "o3")
        wg1_sb = [load_wg(wg1, 0, "wg1lo")]
        raw1 = [load_weight(w1, a, 1, a) for a in range(2)]
        o5 = load_list(offs5, "o5")
        wg1_sb.append(load_wg(wg1, 1, "wg1hi"))
        w4w = new_tile([P, 2, N], U32, "w4w")
        nc.sync.dma_start(w4w[:].bitcast(I32), w4_words.rearrange("a p c i -> p a (c i)").bitcast(I32))
        load_scales(w4s, w4_scales, nc.sync)

        pick_slots = ("raw2", "raw3", "raw0")

        def make_h1(u):
            b, t = divmod(u, PACK)
            cols = slice(t * P, (t + 1) * P)
            acc = psum.tile([P, S], F32, name="acc_h1", tag="pa")
            for a in range(2):
                mx(acc[:], w1c[b][a][:, cols], w1s[b][a][:, cols], v1w[a][:], v1s[a][:], a == 0, a == 1)
            if u == 2:
                bent = new_tile([P, S], F32, "bent", tag="raw1")
            elif u < PACK:
                bent = new_tile([P, S], F32, "bent", bufs=2)
            else:
                bent = new_tile([P, S], F32, "bent", tag=pick_slots[(u - PACK) % 3])
            nc.scalar.activation(bent[:], acc[:], ACT.Tanh)
            lin = psum.tile([P, S], F32, name="lin", tag="pb")
            for jb in range(S // P):
                nc.tensor.transpose(lin[:, jb * P : (jb + 1) * P], lin_t[b][jb][:, t, :], ident[:])
            h1 = new_tile([P, S], F32, "h1", bufs=2)
            if u < 3:
                nc.vector.scalar_tensor_tensor(h1[:], bent[:], gain_sb[:, u : u + 1], lin[:], MULT, ADD)
            else:
                lin_sb = new_tile([P, S], F32, "lin_sb", bufs=2)
                nc.scalar.copy(lin_sb[:], lin[:])
                nc.gpsimd.tensor_scalar(h1[:], bent[:], gain_sb[:, u : u + 1], 0.0, MULT, ADD)
                nc.gpsimd.tensor_tensor(h1[:], h1[:], lin_sb[:], ADD)
            return h1

        xb1 = [new_tile([P, CHUNK, PACK], BF16, "xb1_%d" % c) for c in range(CHUNKS)]

        def round_x(dst, src, u):
            nc.scalar.activation(dst, src, ACT.Identity, bias=neg_base[:, u : u + 1])

        h1 = [make_h1(0), make_h1(1)]
        for u in range(TILES):
            t = u % PACK
            nc.vector.tensor_tensor(pages[u][:].indirect(o3[:]), h1[u][:], wg1_sb[t // 2][:, t % 2, :], MULT)
            if u == 0:
                for a in range(2):
                    quantize_weight(raw1[a], w1c[1][a], w1s[1][a], whole)
            if u == 2:
                lin_t.append(make_lin_t(1))
            if u + 2 < TILES:
                h1.append(make_h1(u + 2))
            if u == 0:
                xb0 = new_tile([P, PICK, PACK], BF16, "xb0", tag="raw1")
            if u < TILES - 1:
                picked = new_tile([P, PICK], F32, "picked", tag=pick_slots[u % 3])
                nc.vector.tensor_copy(picked[:], pages[u][:].indirect(o5[:]))
                if u < PACK:
                    round_x(xb0[:, :, u], picked[:], u)
                else:
                    for c in range(CHUNKS):
                        round_x(xb1[c][:, :, t], picked[:, c * CHUNK : (c + 1) * CHUNK], u)
            if u == PACK + 1:
                x0c = new_tile([P, PICK], U32, "x0c", tag="wg1lo")
                x0s = new_tile([P, PICK], U8, "x0s")
                nc.vector.quantize_mx(
                    out=x0c[:].bitcast(FP8X4), scales=x0s[:], in_=xb0[:].rearrange("p c t -> p (c t)")
                )

        ages_sb = []
        for c, (tag, bufs) in enumerate((("wg2lo", 1), ("wg2hi", 1), ("stage", 2), ("stage", 2))):
            dst = new_tile([P, N // P, CHUNK], F32, "ages_sb", tag=tag, bufs=bufs)
            nc.sync.dma_start(dst[:], ages[:, c * CHUNK : (c + 1) * CHUNK].rearrange("(n p) j -> p n j", p=P))
            ages_sb.append(dst)

        y = []
        for c, tag in enumerate(("pc", "pt", "pa", "pb")):
            cols = slice(c * CHUNK, (c + 1) * CHUNK)
            pair = []
            for h in range(2):
                acc = psum.tile([P, 2, CHUNK], F32, name="acc_y", tag=tag)
                for i in range(2):
                    chans = slice((2 * h + i) * P, (2 * h + i + 1) * P)
                    mx(acc[:, i, :], w4w[:, 0, chans], w4s[:, 0, chans], x0c[:, cols], x0s[:, cols], i == 0, False)
                pair.append(acc)
            y.append(pair)

        last = TILES - 1
        picked = new_tile([P, PICK], F32, "picked", tag=pick_slots[last % 3])
        per_chunk = CHUNK // 16
        for c in range(CHUNKS):
            cols = slice(c * CHUNK, (c + 1) * CHUNK)
            nc.vector.tensor_copy(
                picked[:, cols], pages[last][:].indirect(o5[:, c * per_chunk : (c + 1) * per_chunk])
            )
            round_x(xb1[c][:, :, PACK - 1], picked[:, cols], last)
        for c in range(CHUNKS):
            x1c = new_tile([P, CHUNK], U32, "x1c%d" % c)
            x1s = new_tile([P, CHUNK], U8, "x1s%d" % c)
            nc.vector.quantize_mx(
                out=x1c[:].bitcast(FP8X4), scales=x1s[:], in_=xb1[c][:].rearrange("p c t -> p (c t)")
            )
            for h in range(2):
                for i in range(2):
                    chans = slice((2 * h + i) * P, (2 * h + i + 1) * P)
                    mx(y[c][h][:, i, :], w4w[:, 1, chans], w4s[:, 1, chans], x1c[:], x1s[:], False, i == 1)
        for c in range(CHUNKS):
            cols = slice(c * CHUNK, (c + 1) * CHUNK)
            for h in range(2):
                scored = ages_sb[c][:, 2 * h : 2 * h + 2, :]
                nc.vector.tensor_tensor(scored, y[c][h][:], scored, MULT)
                nc.sync.dma_start(
                    out[2 * h * P : (2 * h + 2) * P, cols].rearrange("(n p) j -> p n j", p=P), scored
                )
